import numpy as np
import ml_dtypes


def mxq(x, axis, fmt="e4m3"):
    dtype, down = {"e4m3": (ml_dtypes.float8_e4m3fn, 7), "e5m2": (ml_dtypes.float8_e5m2, 14)}[fmt]
    v = np.moveaxis(np.asarray(x, np.float32).astype(ml_dtypes.bfloat16).astype(np.float64), axis, -1)
    blocks = v.reshape(v.shape[:-1] + (-1, 32))
    amax = np.abs(blocks).max(-1, keepdims=True)
    byte = np.maximum(np.where(amax > 0, np.frexp(amax)[1] - 1 + 127, 0) - down, 1)
    scale = np.exp2(byte - 127.0)
    codes = (blocks / scale).astype(np.float32).astype(dtype).astype(np.float64)
    return np.moveaxis((codes * scale).reshape(v.shape), -1, axis)


WIDE = False


def mx_kscale(k):
    if not WIDE:
        return np.ones(k)
    levels = np.array([30, -30])
    if k % 512:
        return np.exp2(np.random.permutation(np.resize(levels, k // 32))).repeat(32)
    a = np.empty((k // 512, 16))
    for p in range(k // 512):
        a[p, :8] = np.random.permutation(np.resize(levels, 8))
        for g in range(8):
            far = levels[np.abs(levels - a[p, g]) >= 10]
            a[p, g + 8] = far[np.random.randint(len(far))]
    return np.exp2(a.ravel()).repeat(32)


def f64(x):
    return np.asarray(x).astype(np.float64)


def striped(idx):
    return np.tile(np.asarray(idx).reshape(-1, 16).T, (8, 1)).astype(np.uint16)


def unstriped(offs):
    return offs[:16].T.reshape(-1).astype(np.int64)


E2M1 = np.array([0.0, 0.5, 1.0, 1.5, 2.0, 3.0, 4.0, 6.0, -0.0, -0.5, -1.0, -1.5, -2.0, -3.0, -4.0, -6.0])


def pack_weight(w, fmt):
    k, n = w.shape
    w = f64(np.asarray(w, np.float32).astype(ml_dtypes.bfloat16)).reshape(k // 32, 32, n)
    amax = np.abs(w).max(1)
    if fmt in ("e4m3", "e5m2"):
        byte = np.frexp(amax)[1] - 1 + 127 - (7 if fmt == "e4m3" else 14)
    else:
        mant, ex = np.frexp(amax / 6.0)
        byte = np.where(mant > 0.5, ex, ex - 1) + 127
    byte = np.clip(np.where(amax > 0, byte, 1), 1, 254)
    scaled = (w * np.exp2(127.0 - byte)[:, None, :]).reshape(k, n).astype(np.float32)
    by_word = np.ascontiguousarray(scaled.reshape(k // 512, 128, 4, n).transpose(0, 1, 3, 2))
    if fmt in ("e4m3", "e5m2"):
        words = by_word.astype(ml_dtypes.float8_e4m3fn if fmt == "e4m3" else ml_dtypes.float8_e5m2).view(np.uint8)
    else:
        c = by_word.astype(ml_dtypes.float4_e2m1fn).view(np.uint8) & 0xF
        words = (c[..., 0::2] | (c[..., 1::2] << 4)).reshape(k // 512, 128, 2 * n)
    return np.ascontiguousarray(words), np.ascontiguousarray(byte.astype(np.uint8).reshape(k // 512, 16, n))


def unpack_weight(words, scales, fmt):
    g, _, n = scales.shape
    words = np.ascontiguousarray(words).reshape(g, 128, n, -1)
    if fmt in ("e4m3", "e5m2"):
        vals = words.view(ml_dtypes.float8_e4m3fn if fmt == "e4m3" else ml_dtypes.float8_e5m2).astype(np.float64)
    else:
        nib = np.empty((g, 128, n, 4), np.uint8)
        nib[..., 0::2] = words & 0xF
        nib[..., 1::2] = words >> 4
        vals = E2M1[nib]
    vals = vals * np.repeat(np.exp2(scales.astype(np.float64) - 127.0), 8, axis=1)[..., None]
    return vals.transpose(0, 1, 3, 2).reshape(g * 512, n)


K, T, J, R, C, O, N = 512, 2048, 256, 512, 512, 256, 256


def setup_inputs():
    n = np.random.standard_normal
    idx = np.random.permutation(T)[:J]
    idx2 = np.random.permutation(T)[:J]
    idx3 = np.random.permutation(C)[:J]
    idx4 = np.random.permutation(C)[:J]
    idx5 = np.random.permutation(C)[:O]
    idx6 = np.random.permutation(C)[:O]
    fk = mx_kscale(K)
    fr = mx_kscale(R)
    xtp = pack_weight(n((K, T)) / fk[:, None], "e5m2")
    wp = pack_weight(n((K, R)) * 1 / np.sqrt(K) * fk[:, None] * fr, "e2m1")
    wbp = pack_weight(n((R, N)) * 1 / np.sqrt(R) / fr[:, None], "e2m1")
    return {
        "xt_words": xtp[0],
        "xt_scales": xtp[1],
        "w_words": wp[0],
        "w_scales": wp[1],
        "wb_words": wbp[0],
        "wb_scales": wbp[1],
        "offs": striped(idx),
        "offs2": striped(idx2),
        "offs3": striped(idx3),
        "offs4": striped(idx4),
        "offs5": striped(idx5),
        "offs6": striped(idx6),
    }


def reference(xt_words, xt_scales, w_words, w_scales, wb_words, wb_scales, offs, offs2, offs3, offs4, offs5, offs6):
    idx = unstriped(offs)
    idx2 = unstriped(offs2)
    idx3 = unstriped(offs3)
    idx4 = unstriped(offs4)
    idx5 = unstriped(offs5)
    idx6 = unstriped(offs6)
    xtu = unpack_weight(xt_words, xt_scales, "e5m2")
    wu = unpack_weight(w_words, w_scales, "e2m1")
    wbu = unpack_weight(wb_words, wb_scales, "e2m1")
    xtidxg = xtu[:, idx]
    a = wu.T @ xtidxg
    xtidx2g = xtu[:, idx2]
    b = wu.T @ xtidx2g
    pw = np.zeros((R, C))
    pw[:, idx3] = a
    pv = np.zeros((R, C))
    pv[:, idx4] = b
    hid = np.abs(pw[:, idx5] - pv[:, idx6])
    hidq = mxq(hid, 0, "e4m3")
    y = wbu.T @ hidq
    return y

@@ -1,0 +1,184 @@
+from contextlib import ExitStack
+
+import concourse.mybir as mybir
+
+K, T, J, R, C, O, N = 512, 2048, 256, 512, 512, 256, 256
+FLOPS = 2 * K * R * J * 2 + 2 * R * N * O
+
+F32 = mybir.dt.float32
+BF16 = mybir.dt.bfloat16
+I32 = mybir.dt.int32
+U32 = mybir.dt.uint32
+U16 = mybir.dt.uint16
+U8 = mybir.dt.uint8
+E4M3 = mybir.dt.float8_e4m3fn_x4
+E5M2 = mybir.dt.float8_e5m2_x4
+E2M1 = mybir.dt.float4_e2m1fn_x4
+ACT = mybir.ActivationFunctionType
+ALU = mybir.AluOpType
+
+P = 128
+PACK = 4
+HALF = O // 2
+
+
+def load_scale_rows(queue, plane, rows, quadrants=range(4)):
+    for q in quadrants:
+        queue.dma_start(out=plane[32 * q : 32 * q + 4, :].bitcast(I32), in_=rows[4 * q : 4 * q + 4, :].bitcast(I32))
+
+
+def tile_list_tied_twoboards_one_plain_kernel(
+    tc, xt_words, xt_scales, w_words, w_scales, wb_words, wb_scales, offs, offs2, offs3, offs4, offs5, offs6, out
+):
+    nc = tc.nc
+    with ExitStack() as ctx:
+        lists = ctx.enter_context(tc.tile_pool(name="lists", bufs=1))
+        sb = ctx.enter_context(tc.tile_pool(name="sb", bufs=1))
+        psum = ctx.enter_context(tc.psum_pool(name="psum", bufs=1))
+
+        idx_a = lists.tile([P, J // 16], U16, name="idx_a")
+        idx_b = lists.tile([P, J // 16], U16, name="idx_b")
+        put_a = lists.tile([P, J // 16], U16, name="put_a")
+        put_b = lists.tile([P, J // 16], U16, name="put_b")
+        read_a = lists.tile([P, O // 16], U16, name="read_a")
+        read_b = lists.tile([P, O // 16], U16, name="read_b")
+
+        x_words = sb.tile([P, T], U32, name="x_words", align_bytes=64)
+        x_plane = sb.tile([P, T], U8, name="x_plane", align_bytes=64)
+        w_raw = sb.tile([P, 2 * R], U8, name="w_raw", align_bytes=64)
+        w_raw_plane = sb.tile([P, R], U8, name="w_raw_plane", align_bytes=64)
+        wb_codes = sb.tile([P, 2 * N], U8, name="wb_codes", align_bytes=64)
+        wb_plane = sb.tile([P, N], U8, name="wb_plane", align_bytes=64)
+
+        nc.vector.memset(x_plane[:].bitcast(I32), 0)
+        nc.vector.memset(w_raw_plane[:].bitcast(I32), 0)
+        nc.vector.memset(wb_plane[:].bitcast(I32), 0)
+
+        nc.sync.dma_start(out=x_words[:].bitcast(I32), in_=xt_words[0].rearrange("p c r -> p (c r)").bitcast(I32))
+        load_scale_rows(nc.sync, x_plane, xt_scales[0])
+        nc.sync.dma_start(idx_b[:], offs2)
+        nc.scalar.dma_start(out=w_raw[:].bitcast(I32), in_=w_words[0].bitcast(I32))
+        load_scale_rows(nc.scalar, w_raw_plane, w_scales[0])
+        nc.sync.dma_start(idx_a[:], offs)
+        nc.sync.dma_start(put_b[:], offs4)
+        nc.sync.dma_start(put_a[:], offs3)
+        nc.sync.dma_start(read_b[:], offs6)
+        nc.sync.dma_start(read_a[:], offs5)
+        nc.sync.dma_start(out=wb_codes[:].bitcast(I32), in_=wb_words[0].bitcast(I32))
+        load_scale_rows(nc.sync, wb_plane, wb_scales[0])
+
+        board_a = [sb.tile([P, C], F32, name=f"board_a{t}") for t in range(PACK)]
+        board_b = [sb.tile([P, C], F32, name=f"board_b{t}") for t in range(PACK)]
+        for t in range(PACK):
+            nc.vector.memset(board_b[t][:], 0.0)
+            nc.vector.memset(board_a[t][:], 0.0)
+
+        w_codes = sb.tile([P, 2 * R], U8, name="w_codes", align_bytes=64)
+        w_plane = sb.tile([P, R], U8, name="w_plane", align_bytes=64)
+        nc.vector.tensor_copy(
+            out=w_codes[:].bitcast(U16).rearrange("p (t m) -> p t m", t=PACK),
+            in_=w_raw[:].bitcast(U16).rearrange("p (m t) -> p t m", t=PACK),
+        )
+        nc.vector.tensor_copy(
+            out=w_plane[:].rearrange("p (t m) -> p t m", t=PACK),
+            in_=w_raw_plane[:].rearrange("p (m t) -> p t m", t=PACK),
+        )
+
+        xa_words = sb.tile([P, J], U32, name="xa_words", align_bytes=64)
+        xb_words = sb.tile([P, J], U32, name="xb_words", align_bytes=64)
+        xa_plane = sb.tile([P, J], U8, name="xa_plane", align_bytes=64)
+        xb_plane = sb.tile([P, J], U8, name="xb_plane", align_bytes=64)
+        nc.vector.tensor_copy(xb_plane[:], x_plane[:].indirect(idx_b[:]))
+        nc.vector.tensor_copy(xa_plane[:], x_plane[:].indirect(idx_a[:]))
+        nc.vector.tensor_copy(xb_words[:], x_words[:].indirect(idx_b[:]))
+        nc.vector.tensor_copy(xa_words[:], x_words[:].indirect(idx_a[:]))
+
+        def first_product(name, t, words, plane):
+            bank = psum.tile([P, J], F32, name=f"{name}{t}")
+            nc.tensor.matmul_mx(
+                out=bank[:],
+                lhsT=w_codes[:, 2 * P * t : 2 * P * (t + 1)].bitcast(E2M1),
+                lhsT_scale=w_plane[:, P * t : P * (t + 1)],
+                rhs=words[:].bitcast(E5M2),
+                rhs_scale=plane[:],
+                start=True,
+                stop=True,
+            )
+            return bank
+
+        bank_a, bank_b = [], []
+        for t in range(PACK):
+            bank_b.append(first_product("bank_b", t, xb_words, xb_plane))
+            bank_a.append(first_product("bank_a", t, xa_words, xa_plane))
+
+        a_sb = [sb.tile([P, J], F32, name=f"a_sb{t}") for t in range(PACK)]
+        b_sb = [sb.tile([P, J], F32, name=f"b_sb{t}") for t in range(PACK)]
+        picked_b = [sb.tile([P, O], F32, name=f"picked_b{t}") for t in range(PACK)]
+        diff = [sb.tile([P, 2, O], F32, name=f"diff{u}") for u in range(2)]
+        hid = [sb.tile([P, HALF, PACK], BF16, name=f"hid{c}", align_bytes=64) for c in range(2)]
+        last = PACK - 1
+
+        def pick_b(t, lo, hi):
+            nc.scalar.activation(picked_b[t][:, lo:hi], board_b[t][:].indirect(read_b[:, lo // 16 : hi // 16]), ACT.Copy)
+
+        def subtract(t, lo, hi):
+            nc.vector.tensor_tensor(
+                diff[t // 2][:, t % 2, lo:hi],
+                board_a[t][:].indirect(read_a[:, lo // 16 : hi // 16]),
+                picked_b[t][:, lo:hi],
+                ALU.subtract,
+            )
+
+        def magnitude(u, c):
+            nc.scalar.activation(
+                hid[c][:, :, 2 * u : 2 * u + 2],
+                diff[u][:, :, HALF * c : HALF * (c + 1)].rearrange("p e o -> p o e"),
+                ACT.Abs,
+            )
+
+        nc.vector.tensor_copy(a_sb[0][:], bank_a[0][:])
+        nc.scalar.copy(b_sb[0][:], bank_b[0][:])
+        for t in range(PACK):
+            nc.scalar.activation(board_b[t][:].indirect(put_b[:]), b_sb[t][:], ACT.Copy)
+            if t < last:
+                nc.scalar.copy(b_sb[t + 1][:], bank_b[t + 1][:])
+                nc.vector.tensor_copy(a_sb[t + 1][:], bank_a[t + 1][:])
+                pick_b(t, 0, O)
+            nc.vector.tensor_copy(board_a[t][:].indirect(put_a[:]), a_sb[t][:])
+            if t > 0:
+                subtract(t - 1, 0, O)
+        for c in range(2):
+            pick_b(last, HALF * c, HALF * (c + 1))
+        for c in range(2):
+            subtract(last, HALF * c, HALF * (c + 1))
+        for u in range(2):
+            for c in range(2):
+                magnitude(u, c)
+
+        for c in range(2):
+            hid_codes = sb.tile([P, HALF], U32, name=f"hid_codes{c}", align_bytes=64)
+            hid_plane = sb.tile([P, HALF], U8, name=f"hid_plane{c}", align_bytes=64)
+            nc.vector.quantize_mx(
+                out=hid_codes[:].bitcast(E4M3), scales=hid_plane[:], in_=hid[c][:].rearrange("p o t -> p (o t)")
+            )
+            for h in range(N // P):
+                acc = psum.tile([P, HALF], F32, name=f"acc{c}{h}", tag=f"bank_b{2 * c + h}")
+                nc.tensor.matmul_mx(
+                    out=acc[:],
+                    lhsT=wb_codes[:, 2 * P * h : 2 * P * (h + 1)].bitcast(E2M1),
+                    lhsT_scale=wb_plane[:, P * h : P * (h + 1)],
+                    rhs=hid_codes[:].bitcast(E4M3),
+                    rhs_scale=hid_plane[:],
+                    start=True,
+                    stop=True,
+                )
+                res = sb.tile([P, HALF], F32, name=f"res{c}{h}")
+                rows = out[P * h : P * (h + 1), HALF * c : HALF * (c + 1)]
+                if h == 0:
+                    nc.vector.tensor_copy(res[:], acc[:])
+                else:
+                    nc.scalar.copy(res[:], acc[:])
+                if c == 1 and h == 1:
+                    nc.scalar.dma_start(out=rows, in_=res[:])
+                else:
+                    nc.sync.dma_start(out=rows, in_=res[:])

@@ -47,31 +47,28 @@ def tile_list_tied_twoboards_one_plain_kernel(
         x_plane = sb.tile([P, T], U8, name="x_plane", align_bytes=64)
         w_raw = sb.tile([P, 2 * R], U8, name="w_raw", align_bytes=64)
         w_raw_plane = sb.tile([P, R], U8, name="w_raw_plane", align_bytes=64)
-        wb_codes = sb.tile([P, 2 * N], U8, name="wb_codes", align_bytes=64)
-        wb_plane = sb.tile([P, N], U8, name="wb_plane", align_bytes=64)
 
         nc.vector.memset(x_plane[:].bitcast(I32), 0)
         nc.vector.memset(w_raw_plane[:].bitcast(I32), 0)
-        nc.vector.memset(wb_plane[:].bitcast(I32), 0)
 
-        nc.sync.dma_start(out=x_words[:].bitcast(I32), in_=xt_words[0].rearrange("p c r -> p (c r)").bitcast(I32))
-        load_scale_rows(nc.sync, x_plane, xt_scales[0])
+        load_scale_rows(nc.scalar, x_plane, xt_scales[0], range(3))
         nc.sync.dma_start(idx_b[:], offs2)
-        nc.scalar.dma_start(out=w_raw[:].bitcast(I32), in_=w_words[0].bitcast(I32))
-        load_scale_rows(nc.scalar, w_raw_plane, w_scales[0])
         nc.sync.dma_start(idx_a[:], offs)
+        nc.sync.dma_start(out=w_raw[:].bitcast(I32), in_=w_words[0].bitcast(I32))
         nc.sync.dma_start(put_b[:], offs4)
+        nc.sync.dma_start(out=x_words[:].bitcast(I32), in_=xt_words[0].rearrange("p c r -> p (c r)").bitcast(I32))
+        load_scale_rows(nc.sync, x_plane, xt_scales[0], range(3, 4))
+        load_scale_rows(nc.sync, w_raw_plane, w_scales[0])
         nc.sync.dma_start(put_a[:], offs3)
         nc.sync.dma_start(read_b[:], offs6)
         nc.sync.dma_start(read_a[:], offs5)
-        nc.sync.dma_start(out=wb_codes[:].bitcast(I32), in_=wb_words[0].bitcast(I32))
-        load_scale_rows(nc.sync, wb_plane, wb_scales[0])
 
         board_a = [sb.tile([P, C], F32, name=f"board_a{t}") for t in range(PACK)]
         board_b = [sb.tile([P, C], F32, name=f"board_b{t}") for t in range(PACK)]
         for t in range(PACK):
-            nc.vector.memset(board_b[t][:], 0.0)
-            nc.vector.memset(board_a[t][:], 0.0)
+            engine = nc.vector if t < PACK // 2 else nc.gpsimd
+            engine.memset(board_b[t][:], 0.0)
+            engine.memset(board_a[t][:], 0.0)
 
         w_codes = sb.tile([P, 2 * R], U8, name="w_codes", align_bytes=64)
         w_plane = sb.tile([P, R], U8, name="w_plane", align_bytes=64)
@@ -84,19 +81,23 @@ def tile_list_tied_twoboards_one_plain_kernel(
             in_=w_raw_plane[:].rearrange("p (m t) -> p t m", t=PACK),
         )
 
+        wb_codes = w_raw[:, 0 : 2 * N]
+        wb_plane = w_raw_plane[:, 0:N]
+        nc.sync.dma_start(out=wb_codes.bitcast(I32), in_=wb_words[0].bitcast(I32))
+        load_scale_rows(nc.sync, wb_plane, wb_scales[0])
+
         xa_words = sb.tile([P, J], U32, name="xa_words", align_bytes=64)
         xb_words = sb.tile([P, J], U32, name="xb_words", align_bytes=64)
         xa_plane = sb.tile([P, J], U8, name="xa_plane", align_bytes=64)
         xb_plane = sb.tile([P, J], U8, name="xb_plane", align_bytes=64)
         nc.vector.tensor_copy(xb_plane[:], x_plane[:].indirect(idx_b[:]))
-        nc.vector.tensor_copy(xa_plane[:], x_plane[:].indirect(idx_a[:]))
         nc.vector.tensor_copy(xb_words[:], x_words[:].indirect(idx_b[:]))
+        nc.vector.tensor_copy(xa_plane[:], x_plane[:].indirect(idx_a[:]))
         nc.vector.tensor_copy(xa_words[:], x_words[:].indirect(idx_a[:]))
 
-        def first_product(name, t, words, plane):
-            bank = psum.tile([P, J], F32, name=f"{name}{t}")
+        def first_product(acc, t, words, plane):
             nc.tensor.matmul_mx(
-                out=bank[:],
+                out=acc,
                 lhsT=w_codes[:, 2 * P * t : 2 * P * (t + 1)].bitcast(E2M1),
                 lhsT_scale=w_plane[:, P * t : P * (t + 1)],
                 rhs=words[:].bitcast(E5M2),
@@ -104,15 +105,28 @@ def tile_list_tied_twoboards_one_plain_kernel(
                 start=True,
                 stop=True,
             )
-            return bank
 
-        bank_a, bank_b = [], []
-        for t in range(PACK):
-            bank_b.append(first_product("bank_b", t, xb_words, xb_plane))
-            bank_a.append(first_product("bank_a", t, xa_words, xa_plane))
+        apart = PACK // 2
+        bank_b = [psum.tile([P, J], F32, name=f"bank_b{t}") for t in range(apart)]
+        bank_a = [psum.tile([P, J], F32, name=f"bank_a{t}") for t in range(apart)]
+        bank_ba = [psum.tile([P, 2 * J], F32, name=f"bank_ba{t}") for t in range(apart, PACK)]
+        for t in range(apart):
+            first_product(bank_b[t][:], t, xb_words, xb_plane)
+        for t in range(apart):
+            first_product(bank_a[t][:], t, xa_words, xa_plane)
+        for t in range(apart, PACK):
+            first_product(bank_ba[t - apart][:, 0:J], t, xb_words, xb_plane)
+            first_product(bank_ba[t - apart][:, J : 2 * J], t, xa_words, xa_plane)
 
-        a_sb = [sb.tile([P, J], F32, name=f"a_sb{t}") for t in range(PACK)]
-        b_sb = [sb.tile([P, J], F32, name=f"b_sb{t}") for t in range(PACK)]
+        ba_sb = [sb.tile([P, 2 * J], F32, name=f"ba_sb{t}") for t in range(PACK)]
+
+        def leave_psum(t):
+            if t < apart:
+                nc.scalar.copy(ba_sb[t][:, 0:J], bank_b[t][:])
+                nc.vector.tensor_copy(ba_sb[t][:, J : 2 * J], bank_a[t][:])
+            else:
+                nc.scalar.copy(ba_sb[t][:], bank_ba[t - apart][:])
+
         picked_b = [sb.tile([P, O], F32, name=f"picked_b{t}") for t in range(PACK)]
         diff = [sb.tile([P, 2, O], F32, name=f"diff{u}") for u in range(2)]
         hid = [sb.tile([P, HALF, PACK], BF16, name=f"hid{c}", align_bytes=64) for c in range(2)]
@@ -129,22 +143,13 @@ def tile_list_tied_twoboards_one_plain_kernel(
                 ALU.subtract,
             )
 
-        def magnitude(u, c):
-            nc.scalar.activation(
-                hid[c][:, :, 2 * u : 2 * u + 2],
-                diff[u][:, :, HALF * c : HALF * (c + 1)].rearrange("p e o -> p o e"),
-                ACT.Abs,
-            )
-
-        nc.vector.tensor_copy(a_sb[0][:], bank_a[0][:])
-        nc.scalar.copy(b_sb[0][:], bank_b[0][:])
+        leave_psum(0)
         for t in range(PACK):
-            nc.scalar.activation(board_b[t][:].indirect(put_b[:]), b_sb[t][:], ACT.Copy)
+            nc.scalar.activation(board_b[t][:].indirect(put_b[:]), ba_sb[t][:, 0:J], ACT.Copy)
             if t < last:
-                nc.scalar.copy(b_sb[t + 1][:], bank_b[t + 1][:])
-                nc.vector.tensor_copy(a_sb[t + 1][:], bank_a[t + 1][:])
+                leave_psum(t + 1)
                 pick_b(t, 0, O)
-            nc.vector.tensor_copy(board_a[t][:].indirect(put_a[:]), a_sb[t][:])
+            nc.vector.tensor_copy(board_a[t][:].indirect(put_a[:]), ba_sb[t][:, J : 2 * J])
             if t > 0:
                 subtract(t - 1, 0, O)
         for c in range(2):
@@ -153,7 +158,11 @@ def tile_list_tied_twoboards_one_plain_kernel(
             subtract(last, HALF * c, HALF * (c + 1))
         for u in range(2):
             for c in range(2):
-                magnitude(u, c)
+                nc.scalar.activation(
+                    hid[c][:, :, 2 * u : 2 * u + 2],
+                    diff[u][:, :, HALF * c : HALF * (c + 1)].rearrange("p e o -> p o e"),
+                    ACT.Abs,
+                )
 
         for c in range(2):
             hid_codes = sb.tile([P, HALF], U32, name=f"hid_codes{c}", align_bytes=64)
@@ -162,7 +171,7 @@ def tile_list_tied_twoboards_one_plain_kernel(
                 out=hid_codes[:].bitcast(E4M3), scales=hid_plane[:], in_=hid[c][:].rearrange("p o t -> p (o t)")
             )
             for h in range(N // P):
-                acc = psum.tile([P, HALF], F32, name=f"acc{c}{h}", tag=f"bank_b{2 * c + h}")
+                acc = psum.tile([P, HALF], F32, name=f"acc{c}{h}", tag=f"bank_{'ba'[c]}{h}")
                 nc.tensor.matmul_mx(
                     out=acc[:],
                     lhsT=wb_codes[:, 2 * P * h : 2 * P * (h + 1)].bitcast(E2M1),

from contextlib import ExitStack

import concourse.mybir as mybir

K, T, J, R, C, O, N = 512, 2048, 256, 512, 512, 256, 256
FLOPS = 2 * K * R * J * 2 + 2 * R * N * O

F32 = mybir.dt.float32
BF16 = mybir.dt.bfloat16
I32 = mybir.dt.int32
U32 = mybir.dt.uint32
U16 = mybir.dt.uint16
U8 = mybir.dt.uint8
E4M3 = mybir.dt.float8_e4m3fn_x4
E5M2 = mybir.dt.float8_e5m2_x4
E2M1 = mybir.dt.float4_e2m1fn_x4
ACT = mybir.ActivationFunctionType
ALU = mybir.AluOpType

P = 128
PACK = 4
HALF = O // 2


def load_scale_rows(queue, plane, rows, quadrants=range(4)):
    for q in quadrants:
        queue.dma_start(out=plane[32 * q : 32 * q + 4, :].bitcast(I32), in_=rows[4 * q : 4 * q + 4, :].bitcast(I32))


def tile_list_tied_twoboards_one_plain_kernel(
    tc, xt_words, xt_scales, w_words, w_scales, wb_words, wb_scales, offs, offs2, offs3, offs4, offs5, offs6, out
):
    nc = tc.nc
    with ExitStack() as ctx:
        lists = ctx.enter_context(tc.tile_pool(name="lists", bufs=1))
        sb = ctx.enter_context(tc.tile_pool(name="sb", bufs=1))
        psum = ctx.enter_context(tc.psum_pool(name="psum", bufs=1))

        idx_a = lists.tile([P, J // 16], U16, name="idx_a")
        idx_b = lists.tile([P, J // 16], U16, name="idx_b")
        put_a = lists.tile([P, J // 16], U16, name="put_a")
        put_b = lists.tile([P, J // 16], U16, name="put_b")
        read_a = lists.tile([P, O // 16], U16, name="read_a")
        read_b = lists.tile([P, O // 16], U16, name="read_b")

        x_words = sb.tile([P, T], U32, name="x_words", align_bytes=64)
        x_plane = sb.tile([P, T], U8, name="x_plane", align_bytes=64)
        w_raw = sb.tile([P, 2 * R], U8, name="w_raw", align_bytes=64)
        w_raw_plane = sb.tile([P, R], U8, name="w_raw_plane", align_bytes=64)

        nc.vector.memset(x_plane[:].bitcast(I32), 0)
        nc.vector.memset(w_raw_plane[:].bitcast(I32), 0)

        load_scale_rows(nc.scalar, x_plane, xt_scales[0], range(3))
        nc.sync.dma_start(idx_b[:], offs2)
        nc.sync.dma_start(idx_a[:], offs)
        nc.sync.dma_start(out=w_raw[:].bitcast(I32), in_=w_words[0].bitcast(I32))
        nc.sync.dma_start(put_b[:], offs4)
        nc.sync.dma_start(out=x_words[:].bitcast(I32), in_=xt_words[0].rearrange("p c r -> p (c r)").bitcast(I32))
        load_scale_rows(nc.sync, x_plane, xt_scales[0], range(3, 4))
        load_scale_rows(nc.sync, w_raw_plane, w_scales[0])
        nc.sync.dma_start(put_a[:], offs3)
        nc.sync.dma_start(read_b[:], offs6)
        nc.sync.dma_start(read_a[:], offs5)

        board_a = [sb.tile([P, C], F32, name=f"board_a{t}") for t in range(PACK)]
        board_b = [sb.tile([P, C], F32, name=f"board_b{t}") for t in range(PACK)]
        for t in range(PACK):
            engine = nc.vector if t < PACK // 2 else nc.gpsimd
            engine.memset(board_b[t][:], 0.0)
            engine.memset(board_a[t][:], 0.0)

        w_codes = sb.tile([P, 2 * R], U8, name="w_codes", align_bytes=64)
        w_plane = sb.tile([P, R], U8, name="w_plane", align_bytes=64)
        nc.vector.tensor_copy(
            out=w_codes[:].bitcast(U16).rearrange("p (t m) -> p t m", t=PACK),
            in_=w_raw[:].bitcast(U16).rearrange("p (m t) -> p t m", t=PACK),
        )
        nc.vector.tensor_copy(
            out=w_plane[:].rearrange("p (t m) -> p t m", t=PACK),
            in_=w_raw_plane[:].rearrange("p (m t) -> p t m", t=PACK),
        )

        wb_codes = w_raw[:, 0 : 2 * N]
        wb_plane = w_raw_plane[:, 0:N]
        nc.sync.dma_start(out=wb_codes.bitcast(I32), in_=wb_words[0].bitcast(I32))
        load_scale_rows(nc.sync, wb_plane, wb_scales[0])

        xa_words = sb.tile([P, J], U32, name="xa_words", align_bytes=64)
        xb_words = sb.tile([P, J], U32, name="xb_words", align_bytes=64)
        xa_plane = sb.tile([P, J], U8, name="xa_plane", align_bytes=64)
        xb_plane = sb.tile([P, J], U8, name="xb_plane", align_bytes=64)
        nc.vector.tensor_copy(xb_plane[:], x_plane[:].indirect(idx_b[:]))
        nc.vector.tensor_copy(xb_words[:], x_words[:].indirect(idx_b[:]))
        nc.vector.tensor_copy(xa_plane[:], x_plane[:].indirect(idx_a[:]))
        nc.vector.tensor_copy(xa_words[:], x_words[:].indirect(idx_a[:]))

        def first_product(acc, t, words, plane):
            nc.tensor.matmul_mx(
                out=acc,
                lhsT=w_codes[:, 2 * P * t : 2 * P * (t + 1)].bitcast(E2M1),
                lhsT_scale=w_plane[:, P * t : P * (t + 1)],
                rhs=words[:].bitcast(E5M2),
                rhs_scale=plane[:],
                start=True,
                stop=True,
            )

        apart = PACK // 2
        bank_b = [psum.tile([P, J], F32, name=f"bank_b{t}") for t in range(apart)]
        bank_a = [psum.tile([P, J], F32, name=f"bank_a{t}") for t in range(apart)]
        bank_ba = [psum.tile([P, 2 * J], F32, name=f"bank_ba{t}") for t in range(apart, PACK)]
        for t in range(apart):
            first_product(bank_b[t][:], t, xb_words, xb_plane)
        for t in range(apart):
            first_product(bank_a[t][:], t, xa_words, xa_plane)
        for t in range(apart, PACK):
            first_product(bank_ba[t - apart][:, 0:J], t, xb_words, xb_plane)
            first_product(bank_ba[t - apart][:, J : 2 * J], t, xa_words, xa_plane)

        ba_sb = [sb.tile([P, 2 * J], F32, name=f"ba_sb{t}") for t in range(PACK)]

        def leave_psum(t):
            if t < apart:
                nc.scalar.copy(ba_sb[t][:, 0:J], bank_b[t][:])
                nc.vector.tensor_copy(ba_sb[t][:, J : 2 * J], bank_a[t][:])
            else:
                nc.scalar.copy(ba_sb[t][:], bank_ba[t - apart][:])

        picked_b = [sb.tile([P, O], F32, name=f"picked_b{t}") for t in range(PACK)]
        diff = [sb.tile([P, 2, O], F32, name=f"diff{u}") for u in range(2)]
        hid = [sb.tile([P, HALF, PACK], BF16, name=f"hid{c}", align_bytes=64) for c in range(2)]
        last = PACK - 1

        def pick_b(t, lo, hi):
            nc.scalar.activation(picked_b[t][:, lo:hi], board_b[t][:].indirect(read_b[:, lo // 16 : hi // 16]), ACT.Copy)

        def subtract(t, lo, hi):
            nc.vector.tensor_tensor(
                diff[t // 2][:, t % 2, lo:hi],
                board_a[t][:].indirect(read_a[:, lo // 16 : hi // 16]),
                picked_b[t][:, lo:hi],
                ALU.subtract,
            )

        leave_psum(0)
        for t in range(PACK):
            nc.scalar.activation(board_b[t][:].indirect(put_b[:]), ba_sb[t][:, 0:J], ACT.Copy)
            if t < last:
                leave_psum(t + 1)
                pick_b(t, 0, O)
            nc.vector.tensor_copy(board_a[t][:].indirect(put_a[:]), ba_sb[t][:, J : 2 * J])
            if t > 0:
                subtract(t - 1, 0, O)
        for c in range(2):
            pick_b(last, HALF * c, HALF * (c + 1))
        for c in range(2):
            subtract(last, HALF * c, HALF * (c + 1))
        for u in range(2):
            for c in range(2):
                nc.scalar.activation(
                    hid[c][:, :, 2 * u : 2 * u + 2],
                    diff[u][:, :, HALF * c : HALF * (c + 1)].rearrange("p e o -> p o e"),
                    ACT.Abs,
                )

        for c in range(2):
            hid_codes = sb.tile([P, HALF], U32, name=f"hid_codes{c}", align_bytes=64)
            hid_plane = sb.tile([P, HALF], U8, name=f"hid_plane{c}", align_bytes=64)
            nc.vector.quantize_mx(
                out=hid_codes[:].bitcast(E4M3), scales=hid_plane[:], in_=hid[c][:].rearrange("p o t -> p (o t)")
            )
            for h in range(N // P):
                acc = psum.tile([P, HALF], F32, name=f"acc{c}{h}", tag=f"bank_{'ba'[c]}{h}")
                nc.tensor.matmul_mx(
                    out=acc[:],
                    lhsT=wb_codes[:, 2 * P * h : 2 * P * (h + 1)].bitcast(E2M1),
                    lhsT_scale=wb_plane[:, P * h : P * (h + 1)],
                    rhs=hid_codes[:].bitcast(E4M3),
                    rhs_scale=hid_plane[:],
                    start=True,
                    stop=True,
                )
                res = sb.tile([P, HALF], F32, name=f"res{c}{h}")
                rows = out[P * h : P * (h + 1), HALF * c : HALF * (c + 1)]
                if h == 0:
                    nc.vector.tensor_copy(res[:], acc[:])
                else:
                    nc.scalar.copy(res[:], acc[:])
                if c == 1 and h == 1:
                    nc.scalar.dma_start(out=rows, in_=res[:])
                else:
                    nc.sync.dma_start(out=rows, in_=res[:])
